import numpy as np
import ml_dtypes


def mxq(x, axis, fmt="e4m3"):
    dtype, down = {"e4m3": (ml_dtypes.float8_e4m3fn, 7), "e5m2": (ml_dtypes.float8_e5m2, 14)}[fmt]
    v = np.moveaxis(np.asarray(x, np.float32).astype(ml_dtypes.bfloat16).astype(np.float64), axis, -1)
    blocks = v.reshape(v.shape[:-1] + (-1, 32))
    amax = np.abs(blocks).max(-1, keepdims=True)
    byte = np.maximum(np.where(amax > 0, np.frexp(amax)[1] - 1 + 127, 0) - down, 1)
    scale = np.exp2(byte - 127.0)
    codes = (blocks / scale).astype(np.float32).astype(dtype).astype(np.float64)
    return np.moveaxis((codes * scale).reshape(v.shape), -1, axis)


WIDE = False


def mx_kscale(k):
    if not WIDE:
        return np.ones(k)
    levels = np.array([10, -10, 5, -5, 0])
    if k % 512:
        return np.exp2(np.random.permutation(np.resize(levels, k // 32))).repeat(32)
    a = np.empty((k // 512, 16))
    for p in range(k // 512):
        a[p, :8] = np.random.permutation(np.resize(levels, 8))
        for g in range(8):
            far = levels[np.abs(levels - a[p, g]) >= 10]
            a[p, g + 8] = far[np.random.randint(len(far))]
    return np.exp2(a.ravel()).repeat(32)


def f64(x):
    return np.asarray(x).astype(np.float64)


def striped(idx):
    return np.tile(idx.reshape(-1, 16).T, (8, 1)).astype(np.uint16)


def unstriped(offs):
    return offs[:16].T.reshape(-1).astype(np.int64)


def pack_weight(w):
    k, n = w.shape
    w = f64(np.asarray(w, np.float32).astype(ml_dtypes.bfloat16)).reshape(k // 32, 32, n)
    amax = np.abs(w).max(1)
    byte = np.clip(np.where(amax > 0, np.frexp(amax)[1] - 1 + 127 - 7, 1), 1, 254)
    scaled = (w * np.exp2(127.0 - byte)[:, None, :]).reshape(k, n).astype(np.float32)
    words = np.ascontiguousarray(scaled.reshape(k // 512, 128, 4, n).transpose(0, 1, 3, 2)).astype(ml_dtypes.float8_e4m3fn).view(np.uint8)
    return words, np.ascontiguousarray(byte.astype(np.uint8).reshape(k // 512, 16, n))


def unpack_weight(words, scales):
    g, p, n, _ = words.shape
    vals = np.ascontiguousarray(words).view(ml_dtypes.float8_e4m3fn).astype(np.float64) * np.repeat(np.exp2(scales.astype(np.float64) - 127.0), 8, axis=1)[..., None]
    return vals.transpose(0, 1, 3, 2).reshape(g * 512, n)


def planes(y):
    n, m = y.shape
    v = y.astype(np.float32).astype(ml_dtypes.bfloat16).astype(np.float64).reshape(n // 32, 32, m)
    top = np.abs(v).max(1)
    byte = np.clip(np.where(top > 0, np.frexp(top)[1] - 1 + 127 - 7, 1), 1, 254)
    codes = (v * np.exp2(127.0 - byte)[:, None, :]).reshape(n, m).astype(np.float32).astype(ml_dtypes.float8_e4m3fn).view(np.uint8)
    words = codes.reshape(n // 512, 128, 4, m).transpose(0, 1, 3, 2)
    return np.ascontiguousarray(words), np.ascontiguousarray(byte.astype(np.uint8).reshape(n // 512, 16, m))


K, T, S, V, H, N = 1024, 1024, 512, 256, 512, 512


def setup_inputs():
    n = np.random.standard_normal
    s = mx_kscale(K)[:, None]
    u = mx_kscale(H)
    near = np.random.permutation(S)
    packed_xT = pack_weight(n((K, T)) * s)
    return {
        "x_words": packed_xT[0],
        "x_scales": packed_xT[1],
        "w1": (n((K, H)) / np.sqrt(K) / s * u).astype(np.float32),
        "w2": (n((H, N)) / np.sqrt(H) / u[:, None]).astype(np.float32),
        "w3": (n((H, N)) / np.sqrt(H) / u[:, None]).astype(np.float32),
        "offs": striped(np.random.permutation(T)[:S]),
        "pos1": striped(near[:V]),
        "pos2": striped(near[V:]),
        "pos3": striped(np.random.permutation(S)[:V]),
        "pos4": striped(np.random.permutation(S)[:V]),
    }


def reference(x_words, x_scales, w1, w2, w3, offs, pos1, pos2, pos3, pos4):
    xq = unpack_weight(x_words, x_scales)[:, unstriped(offs)]
    h = mxq(f64(w1), 0, "e4m3").T @ xq
    hq = mxq(h, 0, "e4m3")
    y = mxq(f64(w3), 0, "e4m3").T @ hq
    e = np.exp(mxq(f64(w2), 0, "e4m3").T @ hq)
    e0 = e[:, unstriped(pos1)]
    e1 = e[:, unstriped(pos2)]
    e2 = e[:, unstriped(pos3)]
    e3 = e[:, unstriped(pos4)]
    num = y[:, unstriped(pos1)] * e0 + y[:, unstriped(pos2)] * e1 + y[:, unstriped(pos3)] * e2 + y[:, unstriped(pos4)] * e3
    den = e0 + e1 + e2 + e3
    out_0 = num / den
    return (out_0,) + planes(out_0)

@@ -1,0 +1,294 @@
+from contextlib import ExitStack
+
+import concourse.mybir as mybir
+from concourse.masks import make_identity
+
+K, T, S, V, H, N = 1024, 1024, 512, 256, 512, 512
+FLOPS = 2 * S * (K * H + 2 * H * N)
+
+F32 = mybir.dt.float32
+BF16 = mybir.dt.bfloat16
+I32 = mybir.dt.int32
+U32 = mybir.dt.uint32
+U16 = mybir.dt.uint16
+U8 = mybir.dt.uint8
+FP8X4 = mybir.dt.float8_e4m3fn_x4
+ACT = mybir.ActivationFunctionType
+ALU = mybir.AluOpType
+AX = mybir.AxisListType
+
+P = 128
+PACK = 4
+PASS = P * PACK
+D = 4
+HALF = 128
+
+
+def tile_picked_zrandla_lin_po_kernel(
+    tc, x_words, x_scales, w1, w2, w3, offs, pos1, pos2, pos3, pos4, out_0, out_1, out_2
+):
+    nc = tc.nc
+    with ExitStack() as ctx:
+        keep = ctx.enter_context(tc.tile_pool(name="keep", bufs=1))
+        ring = ctx.enter_context(tc.tile_pool(name="ring", bufs=3))
+        psum = ctx.enter_context(tc.psum_pool(name="psum", bufs=1))
+
+        def bank(b, shape, name):
+            return psum.tile(shape, F32, name=name, tag="bank%d" % b)
+
+        def sb(shape, dtype, name):
+            return keep.tile(shape, dtype, name=name, align_bytes=64)
+
+        def load_rows(w, g, c0, width, name):
+            raw = sb([P, PACK, width], F32, name)
+            nc.sync.dma_start(
+                out=raw[:],
+                in_=w[g * PASS : (g + 1) * PASS, c0 : c0 + width].rearrange("(p j) c -> p j c", j=PACK),
+            )
+            return raw
+
+        def load_words(g):
+            words = sb([P, T], I32, "xw%d" % g)
+            nc.sync.dma_start(out=words[:], in_=x_words[g].rearrange("p n r -> p (n r)").bitcast(I32))
+            return words
+
+        def load_list(src, n, name):
+            lst = keep.tile([P, n // 16], U16, name=name)
+            nc.sync.dma_start(lst[:], src)
+            return lst
+
+        def deal(raw, width, on_scalar, name, tag=None):
+            dealt = keep.tile([P, PACK, width // PACK, PACK], BF16, name=name, tag=tag or name, align_bytes=64)
+            dst = dealt[:].rearrange("p t m j -> p m j t")
+            src = raw.rearrange("p j (m t) -> p m j t", t=PACK)
+            if on_scalar:
+                nc.scalar.activation(dst, src, ACT.Copy)
+            else:
+                nc.vector.tensor_copy(dst, src)
+            return dealt
+
+        def quantize_half(dealt, half, codes, scales):
+            for t in range(PACK):
+                cols = slice(P * t + 64 * half, P * t + 64 * (half + 1))
+                nc.vector.quantize_mx(
+                    out=codes[:, cols].bitcast(FP8X4),
+                    scales=scales[:, cols],
+                    in_=dealt[:, t].rearrange("p m j -> p (m j)"),
+                )
+
+        def gather(dst, window, offsets, on_scalar):
+            if on_scalar:
+                nc.scalar.activation(dst, window[:].indirect(offsets), ACT.Copy)
+            else:
+                nc.vector.tensor_copy(dst, window[:].indirect(offsets))
+
+        xs = sb([P, T], U8, "xs")
+        nc.gpsimd.memset(xs[:].bitcast(I32), 0)
+        offs_sb = load_list(offs, S, "offs_sb")
+        xw0 = load_words(0)
+        w1_raw0 = load_rows(w1, 0, 0, H, "w1_raw0")
+        for q in range(4):
+            nc.scalar.dma_start(
+                out=xs[32 * q : 32 * q + 8, :].bitcast(I32),
+                in_=x_scales[:, 4 * q : 4 * q + 4, :].bitcast(I32),
+            )
+        xw1 = load_words(1)
+        w1_raw1 = [load_rows(w1, 1, 256 * a, 256, "w1_raw1_%d" % a) for a in range(2)]
+        w2_raw = [load_rows(w2, 0, 256 * a, 256, "w2_raw_%d" % a) for a in range(2)]
+        w3_raw = [load_rows(w3, 0, 256 * a, 256, "w3_raw_%d" % a) for a in range(2)]
+        pos = [load_list(src, V, "pos_sb%d" % d) for d, src in enumerate((pos1, pos2, pos3, pos4))]
+
+        ident = sb([P, P], F32, "ident")
+        make_identity(nc, ident[:])
+
+        xg = [sb([P, S], U32, "xg%d" % g) for g in range(2)]
+        xsg = sb([P, S], U8, "xsg")
+        w1q = [sb([P, H], U32, "w1q%d" % g) for g in range(2)]
+        w1s = [sb([P, H], U8, "w1s%d" % g) for g in range(2)]
+        nc.vector.tensor_copy(xg[0][:], xw0[:].bitcast(U32).indirect(offs_sb[:]))
+        nc.vector.tensor_copy(xsg[:], xs[:].indirect(offs_sb[:]))
+        w1d0 = [deal(w1_raw0[:, :, 256 * a : 256 * (a + 1)], 256, a == 0, "w1d0_%d" % a) for a in range(2)]
+        quantize_half(w1d0[1], 1, w1q[0], w1s[0])
+        nc.vector.tensor_copy(xg[1][:], xw1[:].bitcast(U32).indirect(offs_sb[:]))
+        quantize_half(w1d0[0], 0, w1q[0], w1s[0])
+
+        hb = [bank(c, [P, PACK, P], "hb%d" % c) for c in range(4)]
+
+        def layer1(g):
+            for c in range(4):
+                cols = slice(P * c, P * (c + 1))
+                for t in range(PACK):
+                    wc = slice(P * t, P * (t + 1))
+                    nc.tensor.matmul_mx(
+                        out=hb[c][:, t, :],
+                        lhsT=w1q[g][:, wc].bitcast(FP8X4),
+                        lhsT_scale=w1s[g][:, wc],
+                        rhs=xg[g][:, cols].bitcast(FP8X4),
+                        rhs_scale=xsg[4 * g : P, cols],
+                        start=(g == 0 and t == 0),
+                        stop=(g == 1 and t == PACK - 1),
+                    )
+
+        layer1(0)
+        w1d1 = [deal(w1_raw1[a][:], 256, a == 0, "w1d1_%d" % a) for a in range(2)]
+        for a in range(2):
+            quantize_half(w1d1[a], a, w1q[1], w1s[1])
+        layer1(1)
+
+        w2q = sb([P, N], U32, "w2q")
+        w2s = sb([P, N], U8, "w2s")
+        for a in range(2):
+            dealt = deal(w2_raw[a][:], 256, False, "w2d_%d" % a)
+            quantize_half(dealt, a, w2q, w2s)
+
+        hq = sb([P, S], U32, "hq")
+        hs = sb([P, S], U8, "hs")
+        h16 = [
+            keep.tile([P, 2, P, PACK], BF16, name="h16_%d" % a, tag="stage16_%d" % a, align_bytes=64)
+            for a in range(2)
+        ]
+        for c in range(4):
+            cols = slice(P * c, P * (c + 1))
+            part = h16[c // 2][:, c % 2]
+            nc.scalar.activation(part, hb[c][:].rearrange("p t n -> p n t"), ACT.Copy)
+            nc.vector.quantize_mx(
+                out=hq[:, cols].bitcast(FP8X4),
+                scales=hs[:, cols],
+                in_=part.rearrange("p n t -> p (n t)"),
+            )
+        w3d = [deal(w3_raw[a][:], 256, a == 0, "w3d_%d" % a, "stage16_%d" % a) for a in range(2)]
+
+        def layer2(wq, ws, t, b, name):
+            acc = bank(b, [P, S], name)
+            wc = slice(P * t, P * (t + 1))
+            nc.tensor.matmul_mx(
+                out=acc[:],
+                lhsT=wq[:, wc].bitcast(FP8X4),
+                lhsT_scale=ws[:, wc],
+                rhs=hq[:].bitcast(FP8X4),
+                rhs_scale=hs[:],
+                start=True,
+                stop=True,
+            )
+            return acc
+
+        e = []
+        for t in range(PACK):
+            score = layer2(w2q, w2s, t, 4 + t, "score%d" % t)
+            neg_top = sb([P, 1], F32, "neg_top%d" % t)
+            nc.vector.tensor_reduce(neg_top[:], score[:], axis=AX.X, op=ALU.max, negate=True)
+            e_t = sb([P, S], F32, "e%d" % t)
+            nc.scalar.activation(e_t[:], score[:], ACT.Exp, bias=neg_top[:], scale=1.0)
+            e.append(e_t)
+
+        w3q = sb([P, N], U32, "w3q")
+        w3s = sb([P, N], U8, "w3s")
+        for a in range(2):
+            quantize_half(w3d[a], a, w3q, w3s)
+        feat = [layer2(w3q, w3s, t, 2 + t, "feat%d" % t) for t in range(PACK)]
+
+        den = [bank(b, [P, 2, 2, P], "den%d" % b) for b in range(2)]
+        inv = [sb([P, 2, 2, P], F32, "inv%d" % b) for b in range(2)]
+        ey = [sb([P, S], F32, "ey%d" % t) for t in range(PACK)]
+
+        def weigh(t):
+            nc.vector.tensor_tensor(ey[t][:], feat[t][:], e[t][:], ALU.mult)
+
+        for t in range(PACK):
+            picked = []
+            for d in range(D):
+                g = sb([P, V], F32, "ge%d_%d" % (t, d))
+                gather(g[:], e[t], pos[d][:], d < 2)
+                picked.append(g)
+            for half in range(2):
+                for d in range(D):
+                    nc.tensor.matmul(
+                        den[t // 2][:, t % 2, half, :],
+                        lhsT=picked[d][:, HALF * half : HALF * (half + 1)],
+                        rhs=ident[:],
+                        is_transpose=True,
+                        start=(d == 0),
+                        stop=(d == D - 1),
+                    )
+            if t >= 1:
+                weigh(t - 1)
+            if t % 2 == 1:
+                root = ring.tile([P, 2, 2, P], F32, name="root", tag="gy0", bufs=2, align_bytes=64)
+                nc.scalar.activation(root[:], den[t // 2][:], ACT.Abs_reciprocal_sqrt)
+                nc.scalar.activation(inv[t // 2][:], root[:], ACT.Square)
+        weigh(PACK - 1)
+
+        o32 = sb([P, 2, PACK, HALF], F32, "o32")
+        oq = [sb([P, HALF], I32, "oq%d" % half) for half in range(2)]
+        osc = sb([P, V], U8, "osc")
+        out_rows = out_0.rearrange("(p t) v -> p t v", t=PACK)
+        out_words = out_1[0].rearrange("p v r -> p (v r)").bitcast(I32)
+
+        units = [(t, (0, 1)) for t in range(PACK - 1)] + [(PACK - 1, (0,)), (PACK - 1, (1,))]
+
+        def fetch(u):
+            t, halves = units[u]
+            num = bank(6 + u % 2, [P, len(halves), P], "num%d" % u)
+            picked = []
+            for d in range(D):
+                g = ring.tile([P, len(halves) * HALF], F32, name="gy%d" % d, bufs=2 if d < 2 else 3, align_bytes=64)
+                gather(g[:], ey[t], pos[d][:, 8 * halves[0] : 8 * (halves[-1] + 1)], d < 2)
+                picked.append(g)
+            for i in range(len(halves)):
+                for d in range(D):
+                    nc.tensor.matmul(
+                        num[:, i, :],
+                        lhsT=picked[d][:, HALF * i : HALF * (i + 1)],
+                        rhs=ident[:],
+                        is_transpose=True,
+                        start=(d == 0),
+                        stop=(d == D - 1),
+                    )
+            return num
+
+        def divide(u, num):
+            t, halves = units[u]
+            turned = ring.tile([P, len(halves), P], F32, name="turned", align_bytes=64)
+            nc.vector.tensor_tensor(
+                turned[:], num[:], inv[t // 2][:, t % 2, halves[0] : halves[-1] + 1, :], ALU.mult
+            )
+            back = bank(u % 2, [P, len(halves), HALF], "back%d" % u)
+            for i in range(len(halves)):
+                nc.tensor.transpose(back[:, i, :], turned[:, i, :], ident[:])
+            return back
+
+        def finish(u, back):
+            t, halves = units[u]
+            nc.scalar.copy(o32[:, halves[0] : halves[-1] + 1, t, :], back[:])
+            if t == PACK - 1:
+                half = halves[0]
+                cols = slice(HALF * half, HALF * (half + 1))
+                nc.sync.dma_start(out=out_rows[:, :, cols], in_=o32[:, half])
+                o16 = sb([P, HALF, PACK], BF16, "o16_%d" % half)
+                nc.vector.tensor_copy(
+                    o16[:].rearrange("p (c i) t -> p c t i", i=4),
+                    o32[:, half].rearrange("p t (c i) -> p c t i", i=4),
+                )
+                nc.vector.quantize_mx(
+                    out=oq[half][:].bitcast(FP8X4),
+                    scales=osc[:, cols],
+                    in_=o16[:].rearrange("p v t -> p (v t)"),
+                )
+                nc.sync.dma_start(out=out_words[:, cols], in_=oq[half][:])
+
+        nums = {}
+        backs = {}
+        for u in range(len(units) + 2):
+            if u < len(units):
+                nums[u] = fetch(u)
+            if 1 <= u <= len(units):
+                backs[u - 1] = divide(u - 1, nums[u - 1])
+            if u >= 2:
+                finish(u - 2, backs[u - 2])
+
+        for q in range(4):
+            queue = nc.sync if q % 2 == 0 else nc.scalar
+            queue.dma_start(
+                out=out_2[0, 4 * q : 4 * q + 4, :].bitcast(I32),
+                in_=osc[32 * q : 32 * q + 4, :].bitcast(I32),
+            )

@@ -57,24 +57,22 @@ def tile_picked_zrandla_lin_po_kernel(
             nc.sync.dma_start(lst[:], src)
             return lst
 
-        def deal(raw, width, on_scalar, name, tag=None):
-            dealt = keep.tile([P, PACK, width // PACK, PACK], BF16, name=name, tag=tag or name, align_bytes=64)
-            dst = dealt[:].rearrange("p t m j -> p m j t")
+        def dealt_tile(name, tag):
+            return keep.tile([P, PACK, P, PACK], BF16, name=name, tag=tag, align_bytes=64)
+
+        def deal(dealt, raw, half, on_scalar):
+            dst = dealt[:, :, 64 * half : 64 * (half + 1), :].rearrange("p t m j -> p m j t")
             src = raw.rearrange("p j (m t) -> p m j t", t=PACK)
             if on_scalar:
                 nc.scalar.activation(dst, src, ACT.Copy)
             else:
                 nc.vector.tensor_copy(dst, src)
-            return dealt
 
-        def quantize_half(dealt, half, codes, scales):
-            for t in range(PACK):
-                cols = slice(P * t + 64 * half, P * t + 64 * (half + 1))
-                nc.vector.quantize_mx(
-                    out=codes[:, cols].bitcast(FP8X4),
-                    scales=scales[:, cols],
-                    in_=dealt[:, t].rearrange("p m j -> p (m j)"),
-                )
+        def quantize(codes, scales, values):
+            nc.vector.quantize_mx(out=codes.bitcast(FP8X4), scales=scales, in_=values)
+
+        def quantize_dealt(dealt, codes, scales):
+            quantize(codes[:], scales[:], dealt[:].rearrange("p t m j -> p (t m j)"))
 
         def gather(dst, window, offsets, on_scalar):
             if on_scalar:
@@ -92,11 +90,12 @@ def tile_picked_zrandla_lin_po_kernel(
                 out=xs[32 * q : 32 * q + 8, :].bitcast(I32),
                 in_=x_scales[:, 4 * q : 4 * q + 4, :].bitcast(I32),
             )
+        pos = [load_list(pos1, V, "pos_sb0")]
+        w1_raw1 = load_rows(w1, 1, 0, H, "w1_raw1")
         xw1 = load_words(1)
-        w1_raw1 = [load_rows(w1, 1, 256 * a, 256, "w1_raw1_%d" % a) for a in range(2)]
         w2_raw = [load_rows(w2, 0, 256 * a, 256, "w2_raw_%d" % a) for a in range(2)]
         w3_raw = [load_rows(w3, 0, 256 * a, 256, "w3_raw_%d" % a) for a in range(2)]
-        pos = [load_list(src, V, "pos_sb%d" % d) for d, src in enumerate((pos1, pos2, pos3, pos4))]
+        pos.extend(load_list(src, V, "pos_sb%d" % (d + 1)) for d, src in enumerate((pos2, pos3, pos4)))
 
         ident = sb([P, P], F32, "ident")
         make_identity(nc, ident[:])
@@ -107,10 +106,10 @@ def tile_picked_zrandla_lin_po_kernel(
         w1s = [sb([P, H], U8, "w1s%d" % g) for g in range(2)]
         nc.vector.tensor_copy(xg[0][:], xw0[:].bitcast(U32).indirect(offs_sb[:]))
         nc.vector.tensor_copy(xsg[:], xs[:].indirect(offs_sb[:]))
-        w1d0 = [deal(w1_raw0[:, :, 256 * a : 256 * (a + 1)], 256, a == 0, "w1d0_%d" % a) for a in range(2)]
-        quantize_half(w1d0[1], 1, w1q[0], w1s[0])
-        nc.vector.tensor_copy(xg[1][:], xw1[:].bitcast(U32).indirect(offs_sb[:]))
-        quantize_half(w1d0[0], 0, w1q[0], w1s[0])
+        w1d = [dealt_tile("w1d%d" % g, "w1d%d" % g) for g in range(2)]
+        for half in range(2):
+            deal(w1d[0], w1_raw0[:, :, 256 * half : 256 * (half + 1)], half, half == 0)
+        quantize_dealt(w1d[0], w1q[0], w1s[0])
 
         hb = [bank(c, [P, PACK, P], "hb%d" % c) for c in range(4)]
 
@@ -130,33 +129,37 @@ def tile_picked_zrandla_lin_po_kernel(
                     )
 
         layer1(0)
-        w1d1 = [deal(w1_raw1[a][:], 256, a == 0, "w1d1_%d" % a) for a in range(2)]
-        for a in range(2):
-            quantize_half(w1d1[a], a, w1q[1], w1s[1])
+        for half in range(2):
+            deal(w1d[1], w1_raw1[:, :, 256 * half : 256 * (half + 1)], half, half == 0)
+        for c in range(4):
+            nc.vector.tensor_copy(
+                xg[1][:, P * c : P * (c + 1)], xw1[:].bitcast(U32).indirect(offs_sb[:, 8 * c : 8 * (c + 1)])
+            )
+            if c == 0:
+                quantize_dealt(w1d[1], w1q[1], w1s[1])
         layer1(1)
 
         w2q = sb([P, N], U32, "w2q")
         w2s = sb([P, N], U8, "w2s")
-        for a in range(2):
-            dealt = deal(w2_raw[a][:], 256, False, "w2d_%d" % a)
-            quantize_half(dealt, a, w2q, w2s)
+        w2d = dealt_tile("w2d", "w1d1")
+        for half in range(2):
+            deal(w2d, w2_raw[half][:], half, False)
 
         hq = sb([P, S], U32, "hq")
         hs = sb([P, S], U8, "hs")
         h16 = [
-            keep.tile([P, 2, P, PACK], BF16, name="h16_%d" % a, tag="stage16_%d" % a, align_bytes=64)
-            for a in range(2)
+            keep.tile([P, 2, P, PACK], BF16, name="h16_%d" % a, tag="h16_%d" % a, align_bytes=64) for a in range(2)
         ]
-        for c in range(4):
-            cols = slice(P * c, P * (c + 1))
-            part = h16[c // 2][:, c % 2]
-            nc.scalar.activation(part, hb[c][:].rearrange("p t n -> p n t"), ACT.Copy)
-            nc.vector.quantize_mx(
-                out=hq[:, cols].bitcast(FP8X4),
-                scales=hs[:, cols],
-                in_=part.rearrange("p n t -> p (n t)"),
-            )
-        w3d = [deal(w3_raw[a][:], 256, a == 0, "w3d_%d" % a, "stage16_%d" % a) for a in range(2)]
+        for a in range(2):
+            for c in range(2):
+                nc.scalar.activation(h16[a][:, c], hb[2 * a + c][:].rearrange("p t n -> p n t"), ACT.Copy)
+            cols = slice(256 * a, 256 * (a + 1))
+            quantize(hq[:, cols], hs[:, cols], h16[a][:].rearrange("p c n t -> p (c n t)"))
+            if a == 0:
+                quantize_dealt(w2d, w2q, w2s)
+        w3d = dealt_tile("w3d", "h16_0")
+        for half in range(2):
+            deal(w3d, w3_raw[half][:], half, True)
 
         def layer2(wq, ws, t, b, name):
             acc = bank(b, [P, S], name)
@@ -183,8 +186,7 @@ def tile_picked_zrandla_lin_po_kernel(
 
         w3q = sb([P, N], U32, "w3q")
         w3s = sb([P, N], U8, "w3s")
-        for a in range(2):
-            quantize_half(w3d[a], a, w3q, w3s)
+        quantize_dealt(w3d, w3q, w3s)
         feat = [layer2(w3q, w3s, t, 2 + t, "feat%d" % t) for t in range(PACK)]
 
         den = [bank(b, [P, 2, 2, P], "den%d" % b) for b in range(2)]
@@ -194,10 +196,10 @@ def tile_picked_zrandla_lin_po_kernel(
         def weigh(t):
             nc.vector.tensor_tensor(ey[t][:], feat[t][:], e[t][:], ALU.mult)
 
-        for t in range(PACK):
+        def sum_scores(t):
             picked = []
             for d in range(D):
-                g = sb([P, V], F32, "ge%d_%d" % (t, d))
+                g = ring.tile([P, V], F32, name="picked%d" % d, align_bytes=64)
                 gather(g[:], e[t], pos[d][:], d < 2)
                 picked.append(g)
             for half in range(2):
@@ -210,13 +212,11 @@ def tile_picked_zrandla_lin_po_kernel(
                         start=(d == 0),
                         stop=(d == D - 1),
                     )
-            if t >= 1:
-                weigh(t - 1)
-            if t % 2 == 1:
-                root = ring.tile([P, 2, 2, P], F32, name="root", tag="gy0", bufs=2, align_bytes=64)
-                nc.scalar.activation(root[:], den[t // 2][:], ACT.Abs_reciprocal_sqrt)
-                nc.scalar.activation(inv[t // 2][:], root[:], ACT.Square)
-        weigh(PACK - 1)
+
+        def invert(b):
+            root = sb([P, 2, 2, P], F32, "root%d" % b)
+            nc.scalar.activation(root[:], den[b][:], ACT.Abs_reciprocal_sqrt)
+            nc.scalar.activation(inv[b][:], root[:], ACT.Square)
 
         o32 = sb([P, 2, PACK, HALF], F32, "o32")
         oq = [sb([P, HALF], I32, "oq%d" % half) for half in range(2)]
@@ -228,21 +228,23 @@ def tile_picked_zrandla_lin_po_kernel(
 
         def fetch(u):
             t, halves = units[u]
-            num = bank(6 + u % 2, [P, len(halves), P], "num%d" % u)
-            picked = []
-            for d in range(D):
-                g = ring.tile([P, len(halves) * HALF], F32, name="gy%d" % d, bufs=2 if d < 2 else 3, align_bytes=64)
-                gather(g[:], ey[t], pos[d][:, 8 * halves[0] : 8 * (halves[-1] + 1)], d < 2)
-                picked.append(g)
+            num = bank((6, 7, 2, 3)[u % 4], [P, len(halves), P], "num%d" % u)
+            offsets = [pos[d][:, 8 * halves[0] : 8 * (halves[-1] + 1)] for d in range(D)]
+            picked = [
+                ring.tile([P, len(halves) * HALF], F32, name="picked%d" % d, align_bytes=64) for d in range(D)
+            ]
+            for d in range(2):
+                gather(picked[d][:], ey[t], offsets[d], True)
+                nc.vector.tensor_tensor(picked[d + 2][:], ey[t][:].indirect(offsets[d + 2]), picked[d][:], ALU.add)
             for i in range(len(halves)):
-                for d in range(D):
+                for d in range(2):
                     nc.tensor.matmul(
                         num[:, i, :],
-                        lhsT=picked[d][:, HALF * i : HALF * (i + 1)],
+                        lhsT=picked[d + 2][:, HALF * i : HALF * (i + 1)],
                         rhs=ident[:],
                         is_transpose=True,
                         start=(d == 0),
-                        stop=(d == D - 1),
+                        stop=(d == 1),
                     )
             return num
 
@@ -252,7 +254,7 @@ def tile_picked_zrandla_lin_po_kernel(
             nc.vector.tensor_tensor(
                 turned[:], num[:], inv[t // 2][:, t % 2, halves[0] : halves[-1] + 1, :], ALU.mult
             )
-            back = bank(u % 2, [P, len(halves), HALF], "back%d" % u)
+            back = bank((0, 1, 4, 5)[u % 4], [P, len(halves), HALF], "back%d" % u)
             for i in range(len(halves)):
                 nc.tensor.transpose(back[:, i, :], turned[:, i, :], ident[:])
             return back
@@ -269,18 +271,24 @@ def tile_picked_zrandla_lin_po_kernel(
                     o16[:].rearrange("p (c i) t -> p c t i", i=4),
                     o32[:, half].rearrange("p t (c i) -> p c t i", i=4),
                 )
-                nc.vector.quantize_mx(
-                    out=oq[half][:].bitcast(FP8X4),
-                    scales=osc[:, cols],
-                    in_=o16[:].rearrange("p v t -> p (v t)"),
-                )
+                quantize(oq[half][:], osc[:, cols], o16[:].rearrange("p v t -> p (v t)"))
                 nc.sync.dma_start(out=out_words[:, cols], in_=oq[half][:])
 
+        sum_scores(0)
+        sum_scores(1)
+        invert(0)
+        weigh(0)
+        sum_scores(2)
         nums = {}
         backs = {}
         for u in range(len(units) + 2):
             if u < len(units):
                 nums[u] = fetch(u)
+            if u + 1 < PACK:
+                weigh(u + 1)
+            if u == 0:
+                sum_scores(3)
+                invert(1)
             if 1 <= u <= len(units):
                 backs[u - 1] = divide(u - 1, nums[u - 1])
             if u >= 2:

@@ -30,7 +30,6 @@ def tile_picked_zrandla_lin_po_kernel(
     nc = tc.nc
     with ExitStack() as ctx:
         keep = ctx.enter_context(tc.tile_pool(name="keep", bufs=1))
-        ring = ctx.enter_context(tc.tile_pool(name="ring", bufs=3))
         psum = ctx.enter_context(tc.psum_pool(name="psum", bufs=1))
 
         def bank(b, shape, name):
@@ -82,8 +81,8 @@ def tile_picked_zrandla_lin_po_kernel(
 
         xs = sb([P, T], U8, "xs")
         nc.gpsimd.memset(xs[:].bitcast(I32), 0)
-        offs_sb = load_list(offs, S, "offs_sb")
         xw0 = load_words(0)
+        offs_sb = load_list(offs, S, "offs_sb")
         w1_raw0 = load_rows(w1, 0, 0, H, "w1_raw0")
         for q in range(4):
             nc.scalar.dma_start(
@@ -161,46 +160,44 @@ def tile_picked_zrandla_lin_po_kernel(
         for half in range(2):
             deal(w3d, w3_raw[half][:], half, True)
 
-        def layer2(wq, ws, t, b, name):
-            acc = bank(b, [P, S], name)
+        def layer2(acc, wq, ws, t, cols):
             wc = slice(P * t, P * (t + 1))
             nc.tensor.matmul_mx(
-                out=acc[:],
+                out=acc[:, cols],
                 lhsT=wq[:, wc].bitcast(FP8X4),
                 lhsT_scale=ws[:, wc],
-                rhs=hq[:].bitcast(FP8X4),
-                rhs_scale=hs[:],
+                rhs=hq[:, cols].bitcast(FP8X4),
+                rhs_scale=hs[:, cols],
                 start=True,
                 stop=True,
             )
-            return acc
 
+        scores = [bank(4 + t, [P, S], "score%d" % t) for t in range(PACK)]
+        for a in range(2):
+            for t in range(PACK):
+                layer2(scores[t], w2q, w2s, t, slice(256 * a, 256 * (a + 1)))
         e = []
         for t in range(PACK):
-            score = layer2(w2q, w2s, t, 4 + t, "score%d" % t)
+            score = scores[t]
             neg_top = sb([P, 1], F32, "neg_top%d" % t)
             nc.vector.tensor_reduce(neg_top[:], score[:], axis=AX.X, op=ALU.max, negate=True)
             e_t = sb([P, S], F32, "e%d" % t)
             nc.scalar.activation(e_t[:], score[:], ACT.Exp, bias=neg_top[:], scale=1.0)
             e.append(e_t)
 
-        w3q = sb([P, N], U32, "w3q")
+        w3q = keep.tile([P, N], U32, name="w3q", tag="w2q", align_bytes=64)
         w3s = sb([P, N], U8, "w3s")
         quantize_dealt(w3d, w3q, w3s)
-        feat = [layer2(w3q, w3s, t, 2 + t, "feat%d" % t) for t in range(PACK)]
+        feat = [bank(2 + t, [P, S], "feat%d" % t) for t in range(PACK)]
+        for t in range(PACK):
+            layer2(feat[t], w3q, w3s, t, slice(0, S))
 
         den = [bank(b, [P, 2, 2, P], "den%d" % b) for b in range(2)]
-        inv = [sb([P, 2, 2, P], F32, "inv%d" % b) for b in range(2)]
-        ey = [sb([P, S], F32, "ey%d" % t) for t in range(PACK)]
-
-        def weigh(t):
-            nc.vector.tensor_tensor(ey[t][:], feat[t][:], e[t][:], ALU.mult)
-
-        def sum_scores(t):
+        for t in range(PACK):
             picked = []
             for d in range(D):
-                g = ring.tile([P, V], F32, name="picked%d" % d, align_bytes=64)
-                gather(g[:], e[t], pos[d][:], d < 2)
+                g = sb([P, V], F32, "picked%d_%d" % (t, d))
+                gather(g[:], e[t], pos[d][:], d < D - 1 or t == PACK - 1)
                 picked.append(g)
             for half in range(2):
                 for d in range(D):
@@ -213,89 +210,60 @@ def tile_picked_zrandla_lin_po_kernel(
                         stop=(d == D - 1),
                     )
 
-        def invert(b):
-            root = sb([P, 2, 2, P], F32, "root%d" % b)
-            nc.scalar.activation(root[:], den[b][:], ACT.Abs_reciprocal_sqrt)
-            nc.scalar.activation(inv[b][:], root[:], ACT.Square)
+        num = []
+        for pair in range(2):
+            tiles = (2 * pair, 2 * pair + 1)
+            ey = {}
+            for t in tiles:
+                ey[t] = sb([P, S], F32, "ey%d" % t)
+                nc.vector.tensor_tensor(ey[t][:], feat[t][:], e[t][:], ALU.mult)
+            total = {}
+            for d in range(D):
+                for t in tiles:
+                    nxt = sb([P, V], F32, "total%d_%d" % (t, d))
+                    if d == 0:
+                        nc.vector.tensor_copy(nxt[:], ey[t][:].indirect(pos[d][:]))
+                    else:
+                        nc.vector.tensor_tensor(nxt[:], ey[t][:].indirect(pos[d][:]), total[t][:], ALU.add)
+                    total[t] = nxt
+            num.extend(total[t] for t in tiles)
 
-        o32 = sb([P, 2, PACK, HALF], F32, "o32")
-        oq = [sb([P, HALF], I32, "oq%d" % half) for half in range(2)]
-        osc = sb([P, V], U8, "osc")
+        root = [sb([P, 2, 2, P], F32, "root%d" % b) for b in range(2)]
+        inv_turned = [sb([P, 2, 2, P], F32, "inv_turned%d" % b) for b in range(2)]
+        for b in range(2):
+            nc.scalar.activation(root[b][:], den[b][:], ACT.Abs_reciprocal_sqrt)
+        for b in range(2):
+            nc.scalar.activation(inv_turned[b][:], root[b][:], ACT.Square)
+
+        o32 = sb([P, PACK, V], F32, "o32")
         out_rows = out_0.rearrange("(p t) v -> p t v", t=PACK)
-        out_words = out_1[0].rearrange("p v r -> p (v r)").bitcast(I32)
-
-        units = [(t, (0, 1)) for t in range(PACK - 1)] + [(PACK - 1, (0,)), (PACK - 1, (1,))]
-
-        def fetch(u):
-            t, halves = units[u]
-            num = bank((6, 7, 2, 3)[u % 4], [P, len(halves), P], "num%d" % u)
-            offsets = [pos[d][:, 8 * halves[0] : 8 * (halves[-1] + 1)] for d in range(D)]
-            picked = [
-                ring.tile([P, len(halves) * HALF], F32, name="picked%d" % d, align_bytes=64) for d in range(D)
-            ]
-            for d in range(2):
-                gather(picked[d][:], ey[t], offsets[d], True)
-                nc.vector.tensor_tensor(picked[d + 2][:], ey[t][:].indirect(offsets[d + 2]), picked[d][:], ALU.add)
-            for i in range(len(halves)):
-                for d in range(2):
-                    nc.tensor.matmul(
-                        num[:, i, :],
-                        lhsT=picked[d + 2][:, HALF * i : HALF * (i + 1)],
-                        rhs=ident[:],
-                        is_transpose=True,
-                        start=(d == 0),
-                        stop=(d == 1),
-                    )
-            return num
-
-        def divide(u, num):
-            t, halves = units[u]
-            turned = ring.tile([P, len(halves), P], F32, name="turned", align_bytes=64)
-            nc.vector.tensor_tensor(
-                turned[:], num[:], inv[t // 2][:, t % 2, halves[0] : halves[-1] + 1, :], ALU.mult
-            )
-            back = bank((0, 1, 4, 5)[u % 4], [P, len(halves), HALF], "back%d" % u)
-            for i in range(len(halves)):
-                nc.tensor.transpose(back[:, i, :], turned[:, i, :], ident[:])
-            return back
-
-        def finish(u, back):
-            t, halves = units[u]
-            nc.scalar.copy(o32[:, halves[0] : halves[-1] + 1, t, :], back[:])
-            if t == PACK - 1:
-                half = halves[0]
-                cols = slice(HALF * half, HALF * (half + 1))
-                nc.sync.dma_start(out=out_rows[:, :, cols], in_=o32[:, half])
-                o16 = sb([P, HALF, PACK], BF16, "o16_%d" % half)
-                nc.vector.tensor_copy(
-                    o16[:].rearrange("p (c i) t -> p c t i", i=4),
-                    o32[:, half].rearrange("p t (c i) -> p c t i", i=4),
+        for t in range(PACK):
+            inv = bank((6, 7, 2, 3)[t], [P, V], "inv%d" % t)
+            for half in range(2):
+                nc.tensor.transpose(
+                    inv[:, HALF * half : HALF * (half + 1)], inv_turned[t // 2][:, t % 2, half, :], ident[:]
                 )
-                quantize(oq[half][:], osc[:, cols], o16[:].rearrange("p v t -> p (v t)"))
-                nc.sync.dma_start(out=out_words[:, cols], in_=oq[half][:])
+            nc.vector.tensor_tensor(o32[:, t, :], inv[:], num[t][:], ALU.mult)
+            nc.sync.dma_start(out=out_rows[:, t, :], in_=o32[:, t, :])
 
-        sum_scores(0)
-        sum_scores(1)
-        invert(0)
-        weigh(0)
-        sum_scores(2)
-        nums = {}
-        backs = {}
-        for u in range(len(units) + 2):
-            if u < len(units):
-                nums[u] = fetch(u)
-            if u + 1 < PACK:
-                weigh(u + 1)
-            if u == 0:
-                sum_scores(3)
-                invert(1)
-            if 1 <= u <= len(units):
-                backs[u - 1] = divide(u - 1, nums[u - 1])
-            if u >= 2:
-                finish(u - 2, backs[u - 2])
+        osc = sb([P, V], U8, "osc")
+        out_words = out_1[0].rearrange("p v r -> p (v r)").bitcast(I32)
+        o16 = [sb([P, HALF, PACK], BF16, "o16_%d" % half) for half in range(2)]
+        for half in range(2):
+            dst = o16[half][:].rearrange("p (c i) t -> p c t i", i=4)
+            src = o32[:, :, HALF * half : HALF * (half + 1)].rearrange("p t (c i) -> p c t i", i=4)
+            if half == 0:
+                nc.vector.tensor_copy(dst, src)
+            else:
+                nc.scalar.activation(dst, src, ACT.Copy)
+        oq = sb([P, V], I32, "oq")
+        for half in range(2):
+            cols = slice(HALF * half, HALF * (half + 1))
+            quantize(oq[:, cols], osc[:, cols], o16[half][:].rearrange("p v t -> p (v t)"))
+        nc.sync.dma_start(out=out_words, in_=oq[:])
 
         for q in range(4):
-            queue = nc.sync if q % 2 == 0 else nc.scalar
+            queue = nc.sync if q == 0 else nc.scalar
             queue.dma_start(
                 out=out_2[0, 4 * q : 4 * q + 4, :].bitcast(I32),
                 in_=osc[32 * q : 32 * q + 4, :].bitcast(I32),

from contextlib import ExitStack

import concourse.mybir as mybir
from concourse.masks import make_identity

K, T, S, V, H, N = 1024, 1024, 512, 256, 512, 512
FLOPS = 2 * S * (K * H + 2 * H * N)

F32 = mybir.dt.float32
BF16 = mybir.dt.bfloat16
I32 = mybir.dt.int32
U32 = mybir.dt.uint32
U16 = mybir.dt.uint16
U8 = mybir.dt.uint8
FP8X4 = mybir.dt.float8_e4m3fn_x4
ACT = mybir.ActivationFunctionType
ALU = mybir.AluOpType
AX = mybir.AxisListType

P = 128
PACK = 4
PASS = P * PACK
D = 4
HALF = 128


def tile_picked_zrandla_lin_po_kernel(
    tc, x_words, x_scales, w1, w2, w3, offs, pos1, pos2, pos3, pos4, out_0, out_1, out_2
):
    nc = tc.nc
    with ExitStack() as ctx:
        keep = ctx.enter_context(tc.tile_pool(name="keep", bufs=1))
        psum = ctx.enter_context(tc.psum_pool(name="psum", bufs=1))

        def bank(b, shape, name):
            return psum.tile(shape, F32, name=name, tag="bank%d" % b)

        def sb(shape, dtype, name):
            return keep.tile(shape, dtype, name=name, align_bytes=64)

        def load_rows(w, g, c0, width, name):
            raw = sb([P, PACK, width], F32, name)
            nc.sync.dma_start(
                out=raw[:],
                in_=w[g * PASS : (g + 1) * PASS, c0 : c0 + width].rearrange("(p j) c -> p j c", j=PACK),
            )
            return raw

        def load_words(g):
            words = sb([P, T], I32, "xw%d" % g)
            nc.sync.dma_start(out=words[:], in_=x_words[g].rearrange("p n r -> p (n r)").bitcast(I32))
            return words

        def load_list(src, n, name):
            lst = keep.tile([P, n // 16], U16, name=name)
            nc.sync.dma_start(lst[:], src)
            return lst

        def dealt_tile(name, tag):
            return keep.tile([P, PACK, P, PACK], BF16, name=name, tag=tag, align_bytes=64)

        def deal(dealt, raw, half, on_scalar):
            dst = dealt[:, :, 64 * half : 64 * (half + 1), :].rearrange("p t m j -> p m j t")
            src = raw.rearrange("p j (m t) -> p m j t", t=PACK)
            if on_scalar:
                nc.scalar.activation(dst, src, ACT.Copy)
            else:
                nc.vector.tensor_copy(dst, src)

        def quantize(codes, scales, values):
            nc.vector.quantize_mx(out=codes.bitcast(FP8X4), scales=scales, in_=values)

        def quantize_dealt(dealt, codes, scales):
            quantize(codes[:], scales[:], dealt[:].rearrange("p t m j -> p (t m j)"))

        def gather(dst, window, offsets, on_scalar):
            if on_scalar:
                nc.scalar.activation(dst, window[:].indirect(offsets), ACT.Copy)
            else:
                nc.vector.tensor_copy(dst, window[:].indirect(offsets))

        xs = sb([P, T], U8, "xs")
        nc.gpsimd.memset(xs[:].bitcast(I32), 0)
        xw0 = load_words(0)
        offs_sb = load_list(offs, S, "offs_sb")
        w1_raw0 = load_rows(w1, 0, 0, H, "w1_raw0")
        for q in range(4):
            nc.scalar.dma_start(
                out=xs[32 * q : 32 * q + 8, :].bitcast(I32),
                in_=x_scales[:, 4 * q : 4 * q + 4, :].bitcast(I32),
            )
        pos = [load_list(pos1, V, "pos_sb0")]
        w1_raw1 = load_rows(w1, 1, 0, H, "w1_raw1")
        xw1 = load_words(1)
        w2_raw = [load_rows(w2, 0, 256 * a, 256, "w2_raw_%d" % a) for a in range(2)]
        w3_raw = [load_rows(w3, 0, 256 * a, 256, "w3_raw_%d" % a) for a in range(2)]
        pos.extend(load_list(src, V, "pos_sb%d" % (d + 1)) for d, src in enumerate((pos2, pos3, pos4)))

        ident = sb([P, P], F32, "ident")
        make_identity(nc, ident[:])

        xg = [sb([P, S], U32, "xg%d" % g) for g in range(2)]
        xsg = sb([P, S], U8, "xsg")
        w1q = [sb([P, H], U32, "w1q%d" % g) for g in range(2)]
        w1s = [sb([P, H], U8, "w1s%d" % g) for g in range(2)]
        nc.vector.tensor_copy(xg[0][:], xw0[:].bitcast(U32).indirect(offs_sb[:]))
        nc.vector.tensor_copy(xsg[:], xs[:].indirect(offs_sb[:]))
        w1d = [dealt_tile("w1d%d" % g, "w1d%d" % g) for g in range(2)]
        for half in range(2):
            deal(w1d[0], w1_raw0[:, :, 256 * half : 256 * (half + 1)], half, half == 0)
        quantize_dealt(w1d[0], w1q[0], w1s[0])

        hb = [bank(c, [P, PACK, P], "hb%d" % c) for c in range(4)]

        def layer1(g):
            for c in range(4):
                cols = slice(P * c, P * (c + 1))
                for t in range(PACK):
                    wc = slice(P * t, P * (t + 1))
                    nc.tensor.matmul_mx(
                        out=hb[c][:, t, :],
                        lhsT=w1q[g][:, wc].bitcast(FP8X4),
                        lhsT_scale=w1s[g][:, wc],
                        rhs=xg[g][:, cols].bitcast(FP8X4),
                        rhs_scale=xsg[4 * g : P, cols],
                        start=(g == 0 and t == 0),
                        stop=(g == 1 and t == PACK - 1),
                    )

        layer1(0)
        for half in range(2):
            deal(w1d[1], w1_raw1[:, :, 256 * half : 256 * (half + 1)], half, half == 0)
        for c in range(4):
            nc.vector.tensor_copy(
                xg[1][:, P * c : P * (c + 1)], xw1[:].bitcast(U32).indirect(offs_sb[:, 8 * c : 8 * (c + 1)])
            )
            if c == 0:
                quantize_dealt(w1d[1], w1q[1], w1s[1])
        layer1(1)

        w2q = sb([P, N], U32, "w2q")
        w2s = sb([P, N], U8, "w2s")
        w2d = dealt_tile("w2d", "w1d1")
        for half in range(2):
            deal(w2d, w2_raw[half][:], half, False)

        hq = sb([P, S], U32, "hq")
        hs = sb([P, S], U8, "hs")
        h16 = [
            keep.tile([P, 2, P, PACK], BF16, name="h16_%d" % a, tag="h16_%d" % a, align_bytes=64) for a in range(2)
        ]
        for a in range(2):
            for c in range(2):
                nc.scalar.activation(h16[a][:, c], hb[2 * a + c][:].rearrange("p t n -> p n t"), ACT.Copy)
            cols = slice(256 * a, 256 * (a + 1))
            quantize(hq[:, cols], hs[:, cols], h16[a][:].rearrange("p c n t -> p (c n t)"))
            if a == 0:
                quantize_dealt(w2d, w2q, w2s)
        w3d = dealt_tile("w3d", "h16_0")
        for half in range(2):
            deal(w3d, w3_raw[half][:], half, True)

        def layer2(acc, wq, ws, t, cols):
            wc = slice(P * t, P * (t + 1))
            nc.tensor.matmul_mx(
                out=acc[:, cols],
                lhsT=wq[:, wc].bitcast(FP8X4),
                lhsT_scale=ws[:, wc],
                rhs=hq[:, cols].bitcast(FP8X4),
                rhs_scale=hs[:, cols],
                start=True,
                stop=True,
            )

        scores = [bank(4 + t, [P, S], "score%d" % t) for t in range(PACK)]
        for a in range(2):
            for t in range(PACK):
                layer2(scores[t], w2q, w2s, t, slice(256 * a, 256 * (a + 1)))
        e = []
        for t in range(PACK):
            score = scores[t]
            neg_top = sb([P, 1], F32, "neg_top%d" % t)
            nc.vector.tensor_reduce(neg_top[:], score[:], axis=AX.X, op=ALU.max, negate=True)
            e_t = sb([P, S], F32, "e%d" % t)
            nc.scalar.activation(e_t[:], score[:], ACT.Exp, bias=neg_top[:], scale=1.0)
            e.append(e_t)

        w3q = keep.tile([P, N], U32, name="w3q", tag="w2q", align_bytes=64)
        w3s = sb([P, N], U8, "w3s")
        quantize_dealt(w3d, w3q, w3s)
        feat = [bank(2 + t, [P, S], "feat%d" % t) for t in range(PACK)]
        for t in range(PACK):
            layer2(feat[t], w3q, w3s, t, slice(0, S))

        den = [bank(b, [P, 2, 2, P], "den%d" % b) for b in range(2)]
        for t in range(PACK):
            picked = []
            for d in range(D):
                g = sb([P, V], F32, "picked%d_%d" % (t, d))
                gather(g[:], e[t], pos[d][:], d < D - 1 or t == PACK - 1)
                picked.append(g)
            for half in range(2):
                for d in range(D):
                    nc.tensor.matmul(
                        den[t // 2][:, t % 2, half, :],
                        lhsT=picked[d][:, HALF * half : HALF * (half + 1)],
                        rhs=ident[:],
                        is_transpose=True,
                        start=(d == 0),
                        stop=(d == D - 1),
                    )

        num = []
        for pair in range(2):
            tiles = (2 * pair, 2 * pair + 1)
            ey = {}
            for t in tiles:
                ey[t] = sb([P, S], F32, "ey%d" % t)
                nc.vector.tensor_tensor(ey[t][:], feat[t][:], e[t][:], ALU.mult)
            total = {}
            for d in range(D):
                for t in tiles:
                    nxt = sb([P, V], F32, "total%d_%d" % (t, d))
                    if d == 0:
                        nc.vector.tensor_copy(nxt[:], ey[t][:].indirect(pos[d][:]))
                    else:
                        nc.vector.tensor_tensor(nxt[:], ey[t][:].indirect(pos[d][:]), total[t][:], ALU.add)
                    total[t] = nxt
            num.extend(total[t] for t in tiles)

        root = [sb([P, 2, 2, P], F32, "root%d" % b) for b in range(2)]
        inv_turned = [sb([P, 2, 2, P], F32, "inv_turned%d" % b) for b in range(2)]
        for b in range(2):
            nc.scalar.activation(root[b][:], den[b][:], ACT.Abs_reciprocal_sqrt)
        for b in range(2):
            nc.scalar.activation(inv_turned[b][:], root[b][:], ACT.Square)

        o32 = sb([P, PACK, V], F32, "o32")
        out_rows = out_0.rearrange("(p t) v -> p t v", t=PACK)
        for t in range(PACK):
            inv = bank((6, 7, 2, 3)[t], [P, V], "inv%d" % t)
            for half in range(2):
                nc.tensor.transpose(
                    inv[:, HALF * half : HALF * (half + 1)], inv_turned[t // 2][:, t % 2, half, :], ident[:]
                )
            nc.vector.tensor_tensor(o32[:, t, :], inv[:], num[t][:], ALU.mult)
            nc.sync.dma_start(out=out_rows[:, t, :], in_=o32[:, t, :])

        osc = sb([P, V], U8, "osc")
        out_words = out_1[0].rearrange("p v r -> p (v r)").bitcast(I32)
        o16 = [sb([P, HALF, PACK], BF16, "o16_%d" % half) for half in range(2)]
        for half in range(2):
            dst = o16[half][:].rearrange("p (c i) t -> p c t i", i=4)
            src = o32[:, :, HALF * half : HALF * (half + 1)].rearrange("p t (c i) -> p c t i", i=4)
            if half == 0:
                nc.vector.tensor_copy(dst, src)
            else:
                nc.scalar.activation(dst, src, ACT.Copy)
        oq = sb([P, V], I32, "oq")
        for half in range(2):
            cols = slice(HALF * half, HALF * (half + 1))
            quantize(oq[:, cols], osc[:, cols], o16[half][:].rearrange("p v t -> p (v t)"))
        nc.sync.dma_start(out=out_words, in_=oq[:])

        for q in range(4):
            queue = nc.sync if q == 0 else nc.scalar
            queue.dma_start(
                out=out_2[0, 4 * q : 4 * q + 4, :].bitcast(I32),
                in_=osc[32 * q : 32 * q + 4, :].bitcast(I32),
            )
